import numpy as np
import ml_dtypes


def mxq(x, axis, fmt="e4m3"):
    dtype, down = {"e4m3": (ml_dtypes.float8_e4m3fn, 7), "e5m2": (ml_dtypes.float8_e5m2, 14)}[fmt]
    v = np.moveaxis(np.asarray(x, np.float32).astype(ml_dtypes.bfloat16).astype(np.float64), axis, -1)
    blocks = v.reshape(v.shape[:-1] + (-1, 32))
    amax = np.abs(blocks).max(-1, keepdims=True)
    byte = np.maximum(np.where(amax > 0, np.frexp(amax)[1] - 1 + 127, 0) - down, 1)
    scale = np.exp2(byte - 127.0)
    codes = (blocks / scale).astype(np.float32).astype(dtype).astype(np.float64)
    return np.moveaxis((codes * scale).reshape(v.shape), -1, axis)


WIDE = False


def mx_kscale(k):
    if not WIDE:
        return np.ones(k)
    levels = np.array([10, -10, 5, -5, 0])
    if k % 512:
        return np.exp2(np.random.permutation(np.resize(levels, k // 32))).repeat(32)
    a = np.empty((k // 512, 16))
    for p in range(k // 512):
        a[p, :8] = np.random.permutation(np.resize(levels, 8))
        for g in range(8):
            far = levels[np.abs(levels - a[p, g]) >= 10]
            a[p, g + 8] = far[np.random.randint(len(far))]
    return np.exp2(a.ravel()).repeat(32)


def f64(x):
    return np.asarray(x).astype(np.float64)


def striped(idx):
    return np.tile(idx.reshape(-1, 16).T, (8, 1)).astype(np.uint16)


def unstriped(offs):
    return offs[:16].T.reshape(-1).astype(np.int64)


E2M1 = np.array([0.0, 0.5, 1.0, 1.5, 2.0, 3.0, 4.0, 6.0, -0.0, -0.5, -1.0, -1.5, -2.0, -3.0, -4.0, -6.0])


def pack_weight(w, fmt):
    k, n = w.shape
    w = f64(np.asarray(w, np.float32).astype(ml_dtypes.bfloat16)).reshape(k // 32, 32, n)
    amax = np.abs(w).max(1)
    if fmt == "e4m3":
        byte = np.frexp(amax)[1] - 1 + 127 - 7
    else:
        mant, ex = np.frexp(amax / 6.0)
        byte = np.where(mant > 0.5, ex, ex - 1) + 127
    byte = np.clip(np.where(amax > 0, byte, 1), 1, 254)
    scaled = (w * np.exp2(127.0 - byte)[:, None, :]).reshape(k, n).astype(np.float32)
    by_word = np.ascontiguousarray(scaled.reshape(k // 512, 128, 4, n).transpose(0, 1, 3, 2))
    if fmt == "e4m3":
        words = by_word.astype(ml_dtypes.float8_e4m3fn).view(np.uint8)
    else:
        c = by_word.astype(ml_dtypes.float4_e2m1fn).view(np.uint8) & 0xF
        words = (c[..., 0::2] | (c[..., 1::2] << 4)).reshape(k // 512, 128, 2 * n)
    return np.ascontiguousarray(words), np.ascontiguousarray(byte.astype(np.uint8).reshape(k // 512, 16, n))


def unpack_weight(words, scales, fmt):
    g, _, n = scales.shape
    words = np.ascontiguousarray(words).reshape(g, 128, n, -1)
    if fmt == "e4m3":
        vals = words.view(ml_dtypes.float8_e4m3fn).astype(np.float64)
    else:
        nib = np.empty((g, 128, n, 4), np.uint8)
        nib[..., 0::2] = words & 0xF
        nib[..., 1::2] = words >> 4
        vals = E2M1[nib]
    vals = vals * np.repeat(np.exp2(scales.astype(np.float64) - 127.0), 8, axis=1)[..., None]
    return vals.transpose(0, 1, 3, 2).reshape(g * 512, n)


def gelu(v):
    return 0.5 * v * (1.0 + np.tanh(np.sqrt(2.0 / np.pi) * (v + 0.044715 * v**3)))


def twice(P):
    return np.random.permutation(np.repeat(np.arange(P), 2))


def bf(x):
    return np.asarray(x, np.float32).astype(ml_dtypes.bfloat16)


def planes(Y):
    n, m = Y.shape
    b = f64(bf(Y)).reshape(n // 32, 32, m)
    amax = np.abs(b).max(1)
    byte = np.clip(np.where(amax > 0, np.frexp(amax)[1] - 1 + 127 - 7, 1), 1, 254)
    codes = (b * np.exp2(127.0 - byte)[:, None, :]).reshape(n, m).astype(np.float32).astype(ml_dtypes.float8_e4m3fn).view(np.uint8)
    words = codes.reshape(n // 512, 128, 4, m).transpose(0, 1, 3, 2)
    return np.ascontiguousarray(words), np.ascontiguousarray(byte.astype(np.uint8).reshape(n // 512, 16, m))


K, H, T, S, P = 512, 1024, 4096, 1024, 512

def setup_inputs():
    n = np.random.standard_normal
    s = mx_kscale(K)[:, None]
    u = mx_kscale(H)[:, None]
    d = {}
    d["tab_words"], d["tab_scales"] = pack_weight(n((K, T)) * s, "e4m3")
    d["offs"] = striped(np.random.permutation(T)[:S])
    d["pos1"] = striped(np.random.permutation(S)[:P])
    d["pos2"] = striped(np.random.permutation(S)[:P])
    d["pos3"] = striped(twice(P))
    d["w1"] = (1.5 * n((K, H)) / s / K ** 0.5).astype(np.float32)
    d["w2_words"], d["w2_scales"] = pack_weight(1.6 * n((K, H)) / s / K ** 0.5, "e2m1")
    d["w3"] = (n((K, H)) / s * u.T / K ** 0.5).astype(np.float32)
    d["w4_words"], d["w4_scales"] = pack_weight(n((H, H)) / u * u.T / H ** 0.5, "e4m3")
    d["detail"] = (np.exp(0.8 * n((H, 1)) + 0.4 * n((H, S))) / u).astype(np.float32)
    return d

def reference(tab_words, tab_scales, offs, pos1, pos2, pos3, w1, w2_words, w2_scales, w3, w4_words, w4_scales, detail):
    v = unpack_weight(tab_words, tab_scales, "e4m3")[:, unstriped(offs)]
    w2 = unpack_weight(w2_words, w2_scales, "e2m1")
    w4 = unpack_weight(w4_words, w4_scales, "e4m3")
    a = mxq(f64(w1), 0, "e4m3").T @ v
    b = w2.T @ v
    c = mxq(f64(w3), 0, "e4m3").T @ v
    h = c * np.tanh(a) * (b / (1.0 + np.exp(-b)))
    x = h[:, unstriped(pos1)] + h[:, unstriped(pos2)]
    sign = w4.T @ mxq(x, 0, "e4m3")
    y = (sign[:, unstriped(pos3)] - h) * f64(detail)
    words, scales = planes(y)
    return y, words, scales

@@ -1,0 +1,246 @@
+from contextlib import ExitStack
+
+import concourse.mybir as mybir
+
+K, H, T, S, NP = 512, 1024, 4096, 1024, 512
+FLOPS = 2 * (3 * K * H * S + H * H * NP)
+
+F32 = mybir.dt.float32
+BF16 = mybir.dt.bfloat16
+I32 = mybir.dt.int32
+U32 = mybir.dt.uint32
+U16 = mybir.dt.uint16
+U8 = mybir.dt.uint8
+FP8X4 = mybir.dt.float8_e4m3fn_x4
+FP4X4 = mybir.dt.float4_e2m1fn_x4
+ACT = mybir.ActivationFunctionType
+ALU = mybir.AluOpType
+
+P = 128
+PACK = 4
+GROUP = P * PACK
+NG = H // GROUP
+BANK = 512
+CHUNK = 256
+STRIPE = 16
+
+
+def tile_list_sign_phrase_encoder_kernel(
+    tc, tab_words, tab_scales, offs, pos1, pos2, pos3, w1, w2_words, w2_scales, w3, w4_words, w4_scales, detail,
+    out_0, out_1, out_2,
+):
+    nc = tc.nc
+    with ExitStack() as ctx:
+        keep = ctx.enter_context(tc.tile_pool(name="keep", bufs=1))
+        raw = ctx.enter_context(tc.tile_pool(name="raw", bufs=3))
+        work = ctx.enter_context(tc.tile_pool(name="work", bufs=2))
+        ring = ctx.enter_context(tc.tile_pool(name="ring", bufs=3))
+        psum = ctx.enter_context(tc.psum_pool(name="psum", bufs=2))
+
+        def kept(shape, dtype, name):
+            return keep.tile(shape, dtype, name=name, align_bytes=64)
+
+        offs_sb = kept([P, S // STRIPE], U16, "offs_sb")
+        pos1_sb = kept([P, NP // STRIPE], U16, "pos1_sb")
+        pos2_sb = kept([P, NP // STRIPE], U16, "pos2_sb")
+        pos3_sb = kept([P, S // STRIPE], U16, "pos3_sb")
+        tab_w = kept([P, T], U32, "tab_w")
+        tab_s = kept([P, T], U8, "tab_s")
+        v_w = kept([P, S], U32, "v_w")
+        v_s = kept([P, S], U8, "v_s")
+        ws_raw = kept([P, H], U8, "ws_raw")
+        ws = kept([P, H], U8, "ws")
+        w2_raw = kept([P, 2 * H], U8, "w2_raw")
+        w2_q = kept([P, 2 * H], U8, "w2_q")
+        wq = {(n, g): kept([P, GROUP], U32, "wq%d_%d" % (n, g)) for n in (1, 3) for g in range(NG)}
+        wsc = {(n, g): kept([P, GROUP], U8, "wsc%d_%d" % (n, g)) for n in (1, 3) for g in range(NG)}
+        w4_q = [kept([P, H], U32, "w4_q%d" % a) for a in range(NG)]
+        h = [kept([P, S], F32, "h%d" % i) for i in range(NG * PACK)]
+        sign = [kept([P, NP], F32, "sign%d" % i) for i in range(NG * PACK)]
+        det = [kept([P, PACK, S], F32, "det%d" % g) for g in range(NG)]
+        x_q = [kept([P, NP], U32, "x_q%d" % g) for g in range(NG)]
+        x_s = [kept([P, NP], U8, "x_s%d" % g) for g in range(NG)]
+        y_q = [kept([P, S], U32, "y_q%d" % g) for g in range(NG)]
+        y_s = [kept([P, S], U8, "y_s%d" % g) for g in range(NG)]
+
+        nc.vector.memset(tab_s[:].bitcast(I32), 0)
+        nc.vector.memset(ws_raw[:].bitcast(I32), 0)
+
+        def load_weight(w, g):
+            w_raw = raw.tile([P, PACK, GROUP], F32, name="w_raw")
+            nc.sync.dma_start(out=w_raw[:], in_=w[:, g * GROUP : (g + 1) * GROUP].rearrange("(p j) c -> p j c", j=PACK))
+            return w_raw
+
+        def round_weight(copy, w_raw):
+            w_bf = work.tile([P, PACK * GROUP], BF16, name="w_bf", align_bytes=64)
+            copy(
+                out=w_bf[:].rearrange("p (t m j) -> p m j t", t=PACK, j=PACK),
+                in_=w_raw[:].rearrange("p j (m t) -> p m j t", t=PACK),
+            )
+            return w_bf
+
+        def quantise_weight(n, g, w_bf):
+            nc.vector.quantize_mx(out=wq[n, g][:].bitcast(FP8X4), scales=wsc[n, g][:], in_=w_bf[:])
+
+        for q in range(4):
+            nc.scalar.dma_start(out=tab_s[32 * q : 32 * q + 4, :].bitcast(I32), in_=tab_scales[0, 4 * q : 4 * q + 4, :].bitcast(I32))
+        for q in range(4):
+            nc.scalar.dma_start(out=ws_raw[32 * q : 32 * q + 4, :].bitcast(I32), in_=w2_scales[0, 4 * q : 4 * q + 4, :].bitcast(I32))
+        nc.sync.dma_start(offs_sb[:], offs)
+        w1_raw0 = load_weight(w1, 0)
+        nc.sync.dma_start(out=tab_w[:].bitcast(I32), in_=tab_words[0].rearrange("p n i -> p (n i)").bitcast(I32))
+        nc.sync.dma_start(out=w2_raw[:].bitcast(I32), in_=w2_words[0].bitcast(I32))
+        w3_raw0 = load_weight(w3, 0)
+        for q in range(4):
+            nc.scalar.dma_start(out=ws_raw[32 * q + 4 : 32 * q + 12, :].bitcast(I32), in_=w4_scales[:, 4 * q : 4 * q + 4, :].bitcast(I32))
+        nc.sync.dma_start(pos1_sb[:], pos1)
+        nc.sync.dma_start(pos2_sb[:], pos2)
+        w1_raw1 = load_weight(w1, 1)
+        w3_raw1 = load_weight(w3, 1)
+        w4_raw = []
+        for a in range(NG):
+            w4_words_sb = raw.tile([P, H], U32, name="w_raw")
+            nc.sync.dma_start(out=w4_words_sb[:].bitcast(I32), in_=w4_words[a].rearrange("p n i -> p (n i)").bitcast(I32))
+            w4_raw.append(w4_words_sb)
+        nc.sync.dma_start(pos3_sb[:], pos3)
+        for g in range(NG):
+            nc.sync.dma_start(out=det[g][:], in_=detail[g * GROUP : (g + 1) * GROUP, :].rearrange("(p t) c -> p t c", t=PACK))
+
+        quantise_weight(1, 0, round_weight(nc.vector.tensor_copy, w1_raw0))
+        nc.vector.tensor_copy(v_s[:], tab_s[:].indirect(offs_sb[:]))
+        nc.vector.tensor_copy(
+            out=ws[:].rearrange("p (g t m) -> p g m t", g=NG, t=PACK),
+            in_=ws_raw[:].rearrange("p (g m t) -> p g m t", g=NG, t=PACK),
+        )
+        for c in range(S // BANK):
+            lo = c * BANK
+            nc.vector.tensor_copy(v_w[:, lo : lo + BANK], tab_w[:].indirect(offs_sb[:, lo // STRIPE : (lo + BANK) // STRIPE]))
+        for g in range(NG):
+            cols = slice(2 * g * GROUP, 2 * (g + 1) * GROUP)
+            nc.vector.tensor_copy(
+                out=w2_q[:, cols].rearrange("p (t m b) -> p m t b", t=PACK, b=2),
+                in_=w2_raw[:, cols].rearrange("p (m t b) -> p m t b", t=PACK, b=2),
+            )
+        quantise_weight(3, 0, round_weight(nc.vector.tensor_copy, w3_raw0))
+
+        def products(i, c):
+            g, t = divmod(i, PACK)
+            cols = slice(c * BANK, (c + 1) * BANK)
+            rows = slice(t * P, (t + 1) * P)
+            moving = dict(rhs=v_w[:, cols].bitcast(FP8X4), rhs_scale=v_s[:, cols], start=True, stop=True)
+            a_ps = psum.tile([P, BANK], F32, name="a_ps")
+            b_ps = psum.tile([P, BANK], F32, name="b_ps")
+            c_ps = psum.tile([P, BANK], F32, name="c_ps")
+            nc.tensor.matmul_mx(out=a_ps[:], lhsT=wq[1, g][:, rows].bitcast(FP8X4), lhsT_scale=wsc[1, g][:, rows], **moving)
+            nc.tensor.matmul_mx(
+                out=b_ps[:], lhsT=w2_q[:, 2 * i * P : 2 * (i + 1) * P].bitcast(FP4X4), lhsT_scale=ws[:, i * P : (i + 1) * P], **moving
+            )
+            nc.tensor.matmul_mx(out=c_ps[:], lhsT=wq[3, g][:, rows].bitcast(FP8X4), lhsT_scale=wsc[3, g][:, rows], **moving)
+            tanh_a = work.tile([P, BANK], F32, name="tanh_a")
+            silu_b = ring.tile([P, BANK], F32, name="silu_b")
+            nc.scalar.activation(out=tanh_a[:], in_=a_ps[:], func=ACT.Tanh)
+            nc.scalar.activation(out=silu_b[:], in_=b_ps[:], func=ACT.Silu)
+            part = work.tile([P, BANK], F32, name="part")
+            nc.vector.tensor_tensor(out=part[:], in0=c_ps[:], in1=tanh_a[:], op=ALU.mult)
+            return part, silu_b
+
+        def finish_h(i, c, part, silu_b):
+            nc.vector.tensor_tensor(out=h[i][:, c * BANK : (c + 1) * BANK], in0=part[:], in1=silu_b[:], op=ALU.mult)
+
+        x_f = {}
+
+        def pick_start(i):
+            start = work.tile([P, NP], F32, name="start")
+            nc.vector.tensor_copy(start[:], h[i][:].indirect(pos1_sb[:]))
+            return start
+
+        def add_end(i, start):
+            g, t = divmod(i, PACK)
+            if t == 0:
+                x_f[g] = keep.tile([P, PACK, NP], F32, name="x_f")
+            nc.vector.tensor_tensor(out=x_f[g][:, t, :], in0=h[i][:].indirect(pos2_sb[:]), in1=start[:], op=ALU.add)
+
+        def interleave(copy, dst, src):
+            copy(out=dst.rearrange("p (c i t) -> p c t i", i=4, t=PACK), in_=src.rearrange("p t (c i) -> p c t i", i=4))
+
+        def quantise_x(g, copies):
+            for c in range(NP // CHUNK):
+                cols = slice(c * CHUNK, (c + 1) * CHUNK)
+                x_bf = work.tile([P, PACK * CHUNK], BF16, name="x_bf", align_bytes=64)
+                interleave(copies[c], x_bf[:], x_f[g][:, :, cols])
+                nc.vector.quantize_mx(out=x_q[g][:, cols].bitcast(FP8X4), scales=x_s[g][:, cols], in_=x_bf[:])
+
+        def deal_w4(a):
+            nc.scalar.copy(
+                out=w4_q[a][:].rearrange("p (g t m) -> p g m t", g=NG, t=PACK),
+                in_=w4_raw[a][:].rearrange("p (g m t) -> p g m t", g=NG, t=PACK),
+            )
+
+        n_tiles = NG * PACK
+        for i in range(n_tiles + 1):
+            if i < n_tiles:
+                first = products(i, 0)
+            if i > 0:
+                start = pick_start(i - 1)
+            if i < n_tiles:
+                finish_h(i, 0, *first)
+                second = products(i, 1)
+            if i > 0:
+                add_end(i - 1, start)
+            if i < n_tiles:
+                finish_h(i, 1, *second)
+            if i == 1:
+                quantise_weight(1, 1, round_weight(nc.scalar.copy, w1_raw1))
+            if i == 2:
+                quantise_weight(3, 1, round_weight(nc.scalar.copy, w3_raw1))
+            if i == PACK:
+                quantise_x(0, [nc.scalar.copy, nc.scalar.copy])
+            if PACK < i <= PACK + NG:
+                deal_w4(i - PACK - 1)
+        quantise_x(1, [nc.scalar.copy, nc.vector.tensor_copy])
+
+        for i in range(n_tiles):
+            rows = slice(i * P, (i + 1) * P)
+            s_ps = psum.tile([P, NP], F32, name="s_ps")
+            for a in range(NG):
+                nc.tensor.matmul_mx(
+                    out=s_ps[:], lhsT=w4_q[a][:, rows].bitcast(FP8X4), lhsT_scale=ws[4 * (a + 1) :, rows],
+                    rhs=x_q[a][:].bitcast(FP8X4), rhs_scale=x_s[a][:], start=(a == 0), stop=(a == NG - 1),
+                )
+            nc.scalar.copy(out=sign[i][:], in_=s_ps[:])
+
+        def differences(g, c):
+            cols = slice(c * CHUNK, (c + 1) * CHUNK)
+            diff = work.tile([P, PACK, CHUNK], F32, name="diff")
+            places = pos3_sb[:, c * CHUNK // STRIPE : (c + 1) * CHUNK // STRIPE]
+            for t in range(PACK):
+                i = g * PACK + t
+                nc.vector.tensor_tensor(out=diff[:, t, :], in0=sign[i][:].indirect(places), in1=h[i][:, cols], op=ALU.subtract)
+            return diff
+
+        def scale_and_round(g, c, diff):
+            cols = slice(c * CHUNK, (c + 1) * CHUNK)
+            y = ring.tile([P, PACK, CHUNK], F32, name="y")
+            nc.vector.tensor_tensor(out=y[:], in0=diff[:], in1=det[g][:, :, cols], op=ALU.mult)
+            nc.sync.dma_start(out=out_0[g * GROUP : (g + 1) * GROUP, cols].rearrange("(p t) c -> p t c", t=PACK), in_=y[:])
+            y_bf = work.tile([P, PACK * CHUNK], BF16, name="y_bf", align_bytes=64)
+            interleave(nc.scalar.copy, y_bf[:], y[:])
+            return y_bf
+
+        def quantise_y(g, c, y_bf):
+            cols = slice(c * CHUNK, (c + 1) * CHUNK)
+            nc.vector.quantize_mx(out=y_q[g][:, cols].bitcast(FP8X4), scales=y_s[g][:, cols], in_=y_bf[:])
+            nc.sync.dma_start(out=out_1[g].rearrange("p n i -> p (n i)").bitcast(I32)[:, cols], in_=y_q[g][:, cols].bitcast(I32))
+            if c == S // CHUNK - 1:
+                for q in range(4):
+                    nc.scalar.dma_start(out=out_2[g, 4 * q : 4 * q + 4, :].bitcast(I32), in_=y_s[g][32 * q : 32 * q + 4, :].bitcast(I32))
+
+        steps = [(g, c) for g in range(NG) for c in range(S // CHUNK)]
+        diffs, rounded = {}, {}
+        for n in range(len(steps) + 2):
+            if n < len(steps):
+                diffs[n] = differences(*steps[n])
+            if 1 <= n <= len(steps):
+                rounded[n - 1] = scale_and_round(*steps[n - 1], diffs[n - 1])
+            if n >= 2:
+                quantise_y(*steps[n - 2], rounded[n - 2])

@@ -32,7 +32,7 @@ def tile_list_sign_phrase_encoder_kernel(
     nc = tc.nc
     with ExitStack() as ctx:
         keep = ctx.enter_context(tc.tile_pool(name="keep", bufs=1))
-        raw = ctx.enter_context(tc.tile_pool(name="raw", bufs=3))
+        raw = ctx.enter_context(tc.tile_pool(name="raw", bufs=2))
         work = ctx.enter_context(tc.tile_pool(name="work", bufs=2))
         ring = ctx.enter_context(tc.tile_pool(name="ring", bufs=3))
         psum = ctx.enter_context(tc.psum_pool(name="psum", bufs=2))
@@ -44,121 +44,125 @@ def tile_list_sign_phrase_encoder_kernel(
         pos1_sb = kept([P, NP // STRIPE], U16, "pos1_sb")
         pos2_sb = kept([P, NP // STRIPE], U16, "pos2_sb")
         pos3_sb = kept([P, S // STRIPE], U16, "pos3_sb")
-        tab_w = kept([P, T], U32, "tab_w")
         tab_s = kept([P, T], U8, "tab_s")
         v_w = kept([P, S], U32, "v_w")
         v_s = kept([P, S], U8, "v_s")
-        ws_raw = kept([P, H], U8, "ws_raw")
-        ws = kept([P, H], U8, "ws")
-        w2_raw = kept([P, 2 * H], U8, "w2_raw")
+        w2_s = kept([P, H], U8, "w2_s")
+        w4_s = kept([P, H], U8, "w4_s")
         w2_q = kept([P, 2 * H], U8, "w2_q")
         wq = {(n, g): kept([P, GROUP], U32, "wq%d_%d" % (n, g)) for n in (1, 3) for g in range(NG)}
         wsc = {(n, g): kept([P, GROUP], U8, "wsc%d_%d" % (n, g)) for n in (1, 3) for g in range(NG)}
         w4_q = [kept([P, H], U32, "w4_q%d" % a) for a in range(NG)]
         h = [kept([P, S], F32, "h%d" % i) for i in range(NG * PACK)]
         sign = [kept([P, NP], F32, "sign%d" % i) for i in range(NG * PACK)]
-        det = [kept([P, PACK, S], F32, "det%d" % g) for g in range(NG)]
+        part = [kept([P, S], F32, "part%d" % n) for n in range(3)]
         x_q = [kept([P, NP], U32, "x_q%d" % g) for g in range(NG)]
         x_s = [kept([P, NP], U8, "x_s%d" % g) for g in range(NG)]
         y_q = [kept([P, S], U32, "y_q%d" % g) for g in range(NG)]
         y_s = [kept([P, S], U8, "y_s%d" % g) for g in range(NG)]
 
+        w2s_raw = kept([P, H], U8, "small")
+        nc.gpsimd.memset(w2s_raw[:].bitcast(I32), 0)
         nc.vector.memset(tab_s[:].bitcast(I32), 0)
-        nc.vector.memset(ws_raw[:].bitcast(I32), 0)
+        for q in range(4):
+            nc.scalar.dma_start(out=w2s_raw[32 * q : 32 * q + 4, :].bitcast(I32), in_=w2_scales[0, 4 * q : 4 * q + 4, :].bitcast(I32))
 
-        def load_weight(w, g):
-            w_raw = raw.tile([P, PACK, GROUP], F32, name="w_raw")
-            nc.sync.dma_start(out=w_raw[:], in_=w[:, g * GROUP : (g + 1) * GROUP].rearrange("(p j) c -> p j c", j=PACK))
-            return w_raw
+        def load_rows(dst, src):
+            nc.sync.dma_start(out=dst, in_=src.rearrange("(p j) c -> p j c", j=PACK))
 
-        def round_weight(copy, w_raw):
+        def quantise_weight(n, g, copy, w_raw, pieces):
             w_bf = work.tile([P, PACK * GROUP], BF16, name="w_bf", align_bytes=64)
-            copy(
-                out=w_bf[:].rearrange("p (t m j) -> p m j t", t=PACK, j=PACK),
-                in_=w_raw[:].rearrange("p j (m t) -> p m j t", t=PACK),
-            )
-            return w_bf
-
-        def quantise_weight(n, g, w_bf):
+            dealt = w_bf[:].rearrange("p (t m j) -> p m j t", t=PACK, j=PACK)
+            given = w_raw.rearrange("p j (m t) -> p m j t", t=PACK)
+            for u in range(pieces):
+                ms = slice(u * P // pieces, (u + 1) * P // pieces)
+                copy(out=dealt[:, ms], in_=given[:, ms])
             nc.vector.quantize_mx(out=wq[n, g][:].bitcast(FP8X4), scales=wsc[n, g][:], in_=w_bf[:])
 
-        for q in range(4):
-            nc.scalar.dma_start(out=tab_s[32 * q : 32 * q + 4, :].bitcast(I32), in_=tab_scales[0, 4 * q : 4 * q + 4, :].bitcast(I32))
-        for q in range(4):
-            nc.scalar.dma_start(out=ws_raw[32 * q : 32 * q + 4, :].bitcast(I32), in_=w2_scales[0, 4 * q : 4 * q + 4, :].bitcast(I32))
         nc.sync.dma_start(offs_sb[:], offs)
-        w1_raw0 = load_weight(w1, 0)
-        nc.sync.dma_start(out=tab_w[:].bitcast(I32), in_=tab_words[0].rearrange("p n i -> p (n i)").bitcast(I32))
-        nc.sync.dma_start(out=w2_raw[:].bitcast(I32), in_=w2_words[0].bitcast(I32))
-        w3_raw0 = load_weight(w3, 0)
-        for q in range(4):
-            nc.scalar.dma_start(out=ws_raw[32 * q + 4 : 32 * q + 12, :].bitcast(I32), in_=w4_scales[:, 4 * q : 4 * q + 4, :].bitcast(I32))
         nc.sync.dma_start(pos1_sb[:], pos1)
         nc.sync.dma_start(pos2_sb[:], pos2)
-        w1_raw1 = load_weight(w1, 1)
-        w3_raw1 = load_weight(w3, 1)
-        w4_raw = []
-        for a in range(NG):
-            w4_words_sb = raw.tile([P, H], U32, name="w_raw")
-            nc.sync.dma_start(out=w4_words_sb[:].bitcast(I32), in_=w4_words[a].rearrange("p n i -> p (n i)").bitcast(I32))
-            w4_raw.append(w4_words_sb)
         nc.sync.dma_start(pos3_sb[:], pos3)
-        for g in range(NG):
-            nc.sync.dma_start(out=det[g][:], in_=detail[g * GROUP : (g + 1) * GROUP, :].rearrange("(p t) c -> p t c", t=PACK))
+        w2_raw = kept([P, 2 * H], U8, "w2_raw")
+        nc.sync.dma_start(out=w2_raw[:].bitcast(I32), in_=w2_words[0].bitcast(I32))
+        w1_raw0 = raw.tile([P, PACK, GROUP], F32, name="w_raw")
+        load_rows(w1_raw0[:], w1[:, :GROUP])
+        w3_raw0 = raw.tile([P, PACK, GROUP], F32, name="w_raw")
+        load_rows(w3_raw0[:], w3[:, :GROUP])
+        tab_w = kept([P, T], U32, "big")
+        nc.sync.dma_start(out=tab_w[:].bitcast(I32), in_=tab_words[0].rearrange("p n i -> p (n i)").bitcast(I32))
+        for q in range(4):
+            nc.scalar.dma_start(out=tab_s[32 * q : 32 * q + 4, :].bitcast(I32), in_=tab_scales[0, 4 * q : 4 * q + 4, :].bitcast(I32))
 
-        quantise_weight(1, 0, round_weight(nc.vector.tensor_copy, w1_raw0))
-        nc.vector.tensor_copy(v_s[:], tab_s[:].indirect(offs_sb[:]))
-        nc.vector.tensor_copy(
-            out=ws[:].rearrange("p (g t m) -> p g m t", g=NG, t=PACK),
-            in_=ws_raw[:].rearrange("p (g m t) -> p g m t", g=NG, t=PACK),
-        )
-        for c in range(S // BANK):
-            lo = c * BANK
-            nc.vector.tensor_copy(v_w[:, lo : lo + BANK], tab_w[:].indirect(offs_sb[:, lo // STRIPE : (lo + BANK) // STRIPE]))
+        def deal_scales(dst, src):
+            nc.vector.tensor_copy(
+                out=dst.rearrange("p (g t m) -> p g m t", g=NG, t=PACK),
+                in_=src.rearrange("p (g m t) -> p g m t", g=NG, t=PACK),
+            )
+
         for g in range(NG):
             cols = slice(2 * g * GROUP, 2 * (g + 1) * GROUP)
             nc.vector.tensor_copy(
                 out=w2_q[:, cols].rearrange("p (t m b) -> p m t b", t=PACK, b=2),
                 in_=w2_raw[:, cols].rearrange("p (m t b) -> p m t b", t=PACK, b=2),
             )
-        quantise_weight(3, 0, round_weight(nc.vector.tensor_copy, w3_raw0))
+        quantise_weight(1, 0, nc.vector.tensor_copy, w1_raw0[:], 1)
+        quantise_weight(3, 0, nc.vector.tensor_copy, w3_raw0[:], 1)
+        det = {}
+        nc.vector.tensor_copy(v_s[:], tab_s[:].indirect(offs_sb[:]))
+        deal_scales(w2_s[:], w2s_raw[:])
+        for c in range(S // BANK):
+            lo = c * BANK
+            nc.vector.tensor_copy(v_w[:, lo : lo + BANK], tab_w[:].indirect(offs_sb[:, lo // STRIPE : (lo + BANK) // STRIPE]))
+        w_raw1 = kept([P, 2, PACK, GROUP], F32, "big")
+        load_rows(w_raw1[:, 0], w1[:, GROUP:])
+        load_rows(w_raw1[:, 1], w3[:, GROUP:])
 
-        def products(i, c):
-            g, t = divmod(i, PACK)
+        def moving(c):
             cols = slice(c * BANK, (c + 1) * BANK)
-            rows = slice(t * P, (t + 1) * P)
-            moving = dict(rhs=v_w[:, cols].bitcast(FP8X4), rhs_scale=v_s[:, cols], start=True, stop=True)
-            a_ps = psum.tile([P, BANK], F32, name="a_ps")
-            b_ps = psum.tile([P, BANK], F32, name="b_ps")
-            c_ps = psum.tile([P, BANK], F32, name="c_ps")
-            nc.tensor.matmul_mx(out=a_ps[:], lhsT=wq[1, g][:, rows].bitcast(FP8X4), lhsT_scale=wsc[1, g][:, rows], **moving)
-            nc.tensor.matmul_mx(
-                out=b_ps[:], lhsT=w2_q[:, 2 * i * P : 2 * (i + 1) * P].bitcast(FP4X4), lhsT_scale=ws[:, i * P : (i + 1) * P], **moving
-            )
-            nc.tensor.matmul_mx(out=c_ps[:], lhsT=wq[3, g][:, rows].bitcast(FP8X4), lhsT_scale=wsc[3, g][:, rows], **moving)
-            tanh_a = work.tile([P, BANK], F32, name="tanh_a")
-            silu_b = ring.tile([P, BANK], F32, name="silu_b")
-            nc.scalar.activation(out=tanh_a[:], in_=a_ps[:], func=ACT.Tanh)
-            nc.scalar.activation(out=silu_b[:], in_=b_ps[:], func=ACT.Silu)
-            part = work.tile([P, BANK], F32, name="part")
-            nc.vector.tensor_tensor(out=part[:], in0=c_ps[:], in1=tanh_a[:], op=ALU.mult)
-            return part, silu_b
+            return dict(rhs=v_w[:, cols].bitcast(FP8X4), rhs_scale=v_s[:, cols], start=True, stop=True)
 
-        def finish_h(i, c, part, silu_b):
-            nc.vector.tensor_tensor(out=h[i][:, c * BANK : (c + 1) * BANK], in0=part[:], in1=silu_b[:], op=ALU.mult)
+        def gates(i):
+            g, t = divmod(i, PACK)
+            rows = slice(t * P, (t + 1) * P)
+            tanh_a = work.tile([P, S], F32, name="tanh_a")
+            silu_b = work.tile([P, S], F32, name="silu_b")
+            for c in range(S // BANK):
+                cols = slice(c * BANK, (c + 1) * BANK)
+                a_ps = psum.tile([P, BANK], F32, name="a_ps")
+                b_ps = psum.tile([P, BANK], F32, name="b_ps")
+                nc.tensor.matmul_mx(out=a_ps[:], lhsT=wq[1, g][:, rows].bitcast(FP8X4), lhsT_scale=wsc[1, g][:, rows], **moving(c))
+                nc.tensor.matmul_mx(
+                    out=b_ps[:], lhsT=w2_q[:, 2 * i * P : 2 * (i + 1) * P].bitcast(FP4X4), lhsT_scale=w2_s[:, i * P : (i + 1) * P], **moving(c)
+                )
+                nc.scalar.activation(out=tanh_a[:, cols], in_=a_ps[:], func=ACT.Tanh)
+                nc.scalar.activation(out=silu_b[:, cols], in_=b_ps[:], func=ACT.Silu)
+                if i < 2:
+                    engine = nc.vector if i == 0 else nc.gpsimd
+                    engine.tensor_tensor(out=part[i % 3][:, cols], in0=tanh_a[:, cols], in1=silu_b[:, cols], op=ALU.mult)
+            if i >= 2:
+                nc.gpsimd.tensor_tensor(out=part[i % 3][:], in0=tanh_a[:], in1=silu_b[:], op=ALU.mult)
+
+        def finish_h(i, c):
+            g, t = divmod(i, PACK)
+            rows = slice(t * P, (t + 1) * P)
+            cols = slice(c * BANK, (c + 1) * BANK)
+            c_ps = psum.tile([P, BANK], F32, name="c_ps")
+            nc.tensor.matmul_mx(out=c_ps[:], lhsT=wq[3, g][:, rows].bitcast(FP8X4), lhsT_scale=wsc[3, g][:, rows], **moving(c))
+            nc.vector.tensor_tensor(out=h[i][:, cols], in0=c_ps[:], in1=part[i % 3][:, cols], op=ALU.mult)
 
         x_f = {}
 
-        def pick_start(i):
-            start = work.tile([P, NP], F32, name="start")
-            nc.vector.tensor_copy(start[:], h[i][:].indirect(pos1_sb[:]))
-            return start
+        def pick_start(i, lo=0, hi=NP):
+            nc.vector.tensor_copy(part[i % 3][:, lo:hi], h[i][:].indirect(pos1_sb[:, lo // STRIPE : hi // STRIPE]))
 
-        def add_end(i, start):
+        def add_end(i, lo=0, hi=NP):
             g, t = divmod(i, PACK)
             if t == 0:
                 x_f[g] = keep.tile([P, PACK, NP], F32, name="x_f")
-            nc.vector.tensor_tensor(out=x_f[g][:, t, :], in0=h[i][:].indirect(pos2_sb[:]), in1=start[:], op=ALU.add)
+            nc.vector.tensor_tensor(
+                out=x_f[g][:, t, lo:hi], in0=h[i][:].indirect(pos2_sb[:, lo // STRIPE : hi // STRIPE]), in1=part[i % 3][:, lo:hi], op=ALU.add
+            )
 
         def interleave(copy, dst, src):
             copy(out=dst.rearrange("p (c i t) -> p c t i", i=4, t=PACK), in_=src.rearrange("p t (c i) -> p c t i", i=4))
@@ -170,33 +174,51 @@ def tile_list_sign_phrase_encoder_kernel(
                 interleave(copies[c], x_bf[:], x_f[g][:, :, cols])
                 nc.vector.quantize_mx(out=x_q[g][:, cols].bitcast(FP8X4), scales=x_s[g][:, cols], in_=x_bf[:])
 
-        def deal_w4(a):
+        def deal_w4(w4_raw, a):
             nc.scalar.copy(
                 out=w4_q[a][:].rearrange("p (g t m) -> p g m t", g=NG, t=PACK),
-                in_=w4_raw[a][:].rearrange("p (g m t) -> p g m t", g=NG, t=PACK),
+                in_=w4_raw[:, a, :].bitcast(U32).rearrange("p (g m t) -> p g m t", g=NG, t=PACK),
             )
 
         n_tiles = NG * PACK
-        for i in range(n_tiles + 1):
-            if i < n_tiles:
-                first = products(i, 0)
+        gates(0)
+        for i in range(n_tiles):
+            if i + 1 < n_tiles:
+                gates(i + 1)
+            finish_h(i, 0)
             if i > 0:
-                start = pick_start(i - 1)
-            if i < n_tiles:
-                finish_h(i, 0, *first)
-                second = products(i, 1)
+                pick_start(i - 1)
+            finish_h(i, 1)
             if i > 0:
-                add_end(i - 1, start)
-            if i < n_tiles:
-                finish_h(i, 1, *second)
+                add_end(i - 1)
+            if i == 0:
+                quantise_weight(1, 1, nc.scalar.copy, w_raw1[:, 0], 2)
             if i == 1:
-                quantise_weight(1, 1, round_weight(nc.scalar.copy, w1_raw1))
+                quantise_weight(3, 1, nc.scalar.copy, w_raw1[:, 1], 2)
+                w4_stage = kept([P, NG * H + H // 4], I32, "big")
+                w4_raw = w4_stage[:, : NG * H].rearrange("p (a n) -> p a n", a=NG)
+                nc.vector.memset(w4_stage[:, NG * H :], 0)
+                nc.sync.dma_start(out=w4_raw, in_=w4_words.rearrange("a p n i -> p a (n i)").bitcast(I32))
+                for q in range(4):
+                    nc.sync.dma_start(out=w4_stage[32 * q : 32 * q + 8, NG * H :], in_=w4_scales[:, 4 * q : 4 * q + 4, :].bitcast(I32))
             if i == 2:
-                quantise_weight(3, 1, round_weight(nc.scalar.copy, w3_raw1))
+                deal_scales(w4_s[:], w4_stage[:, NG * H :].bitcast(U8))
+                for u in range(2):
+                    det[0, u] = work.tile([P, PACK, BANK], F32, name="w_bf", align_bytes=64)
+                    load_rows(det[0, u][:], detail[:GROUP, u * BANK : (u + 1) * BANK])
+            if i in (2, 3):
+                deal_w4(w4_raw, i - 2)
+            if i == 3:
+                det1 = kept([P, 2, PACK, BANK], F32, "big")
+                for u in range(2):
+                    det[1, u] = det1[:, u]
+                    load_rows(det[1, u], detail[GROUP:, u * BANK : (u + 1) * BANK])
             if i == PACK:
                 quantise_x(0, [nc.scalar.copy, nc.scalar.copy])
-            if PACK < i <= PACK + NG:
-                deal_w4(i - PACK - 1)
+        for lo in range(0, NP, CHUNK):
+            pick_start(n_tiles - 1, lo, lo + CHUNK)
+        for lo in range(0, NP, CHUNK):
+            add_end(n_tiles - 1, lo, lo + CHUNK)
         quantise_x(1, [nc.scalar.copy, nc.vector.tensor_copy])
 
         for i in range(n_tiles):
@@ -204,43 +226,44 @@ def tile_list_sign_phrase_encoder_kernel(
             s_ps = psum.tile([P, NP], F32, name="s_ps")
             for a in range(NG):
                 nc.tensor.matmul_mx(
-                    out=s_ps[:], lhsT=w4_q[a][:, rows].bitcast(FP8X4), lhsT_scale=ws[4 * (a + 1) :, rows],
+                    out=s_ps[:], lhsT=w4_q[a][:, rows].bitcast(FP8X4), lhsT_scale=w4_s[4 * a :, rows],
                     rhs=x_q[a][:].bitcast(FP8X4), rhs_scale=x_s[a][:], start=(a == 0), stop=(a == NG - 1),
                 )
             nc.scalar.copy(out=sign[i][:], in_=s_ps[:])
 
-        def differences(g, c):
-            cols = slice(c * CHUNK, (c + 1) * CHUNK)
-            diff = work.tile([P, PACK, CHUNK], F32, name="diff")
-            places = pos3_sb[:, c * CHUNK // STRIPE : (c + 1) * CHUNK // STRIPE]
+        def differences(g, lo, width):
+            diff = work.tile([P, PACK, width], F32, name="diff")
+            places = pos3_sb[:, lo // STRIPE : (lo + width) // STRIPE]
             for t in range(PACK):
                 i = g * PACK + t
-                nc.vector.tensor_tensor(out=diff[:, t, :], in0=sign[i][:].indirect(places), in1=h[i][:, cols], op=ALU.subtract)
+                nc.vector.tensor_tensor(out=diff[:, t, :], in0=sign[i][:].indirect(places), in1=h[i][:, lo : lo + width], op=ALU.subtract)
             return diff
 
-        def scale_and_round(g, c, diff):
-            cols = slice(c * CHUNK, (c + 1) * CHUNK)
-            y = ring.tile([P, PACK, CHUNK], F32, name="y")
-            nc.vector.tensor_tensor(out=y[:], in0=diff[:], in1=det[g][:, :, cols], op=ALU.mult)
-            nc.sync.dma_start(out=out_0[g * GROUP : (g + 1) * GROUP, cols].rearrange("(p t) c -> p t c", t=PACK), in_=y[:])
-            y_bf = work.tile([P, PACK * CHUNK], BF16, name="y_bf", align_bytes=64)
-            interleave(nc.scalar.copy, y_bf[:], y[:])
+        def scale_and_round(g, lo, width, diff, copy):
+            y = ring.tile([P, PACK, width], F32, name="y")
+            u, at = divmod(lo, BANK)
+            nc.vector.tensor_tensor(out=y[:], in0=diff[:], in1=det[g, u][:, :, at : at + width], op=ALU.mult)
+            nc.sync.dma_start(out=out_0[g * GROUP : (g + 1) * GROUP, lo : lo + width].rearrange("(p t) c -> p t c", t=PACK), in_=y[:])
+            y_bf = work.tile([P, PACK * width], BF16, name="y_bf", align_bytes=64)
+            interleave(copy, y_bf[:], y[:])
             return y_bf
 
-        def quantise_y(g, c, y_bf):
-            cols = slice(c * CHUNK, (c + 1) * CHUNK)
+        def quantise_y(g, lo, width, y_bf):
+            cols = slice(lo, lo + width)
             nc.vector.quantize_mx(out=y_q[g][:, cols].bitcast(FP8X4), scales=y_s[g][:, cols], in_=y_bf[:])
             nc.sync.dma_start(out=out_1[g].rearrange("p n i -> p (n i)").bitcast(I32)[:, cols], in_=y_q[g][:, cols].bitcast(I32))
-            if c == S // CHUNK - 1:
+            if lo + width == S:
                 for q in range(4):
                     nc.scalar.dma_start(out=out_2[g, 4 * q : 4 * q + 4, :].bitcast(I32), in_=y_s[g][32 * q : 32 * q + 4, :].bitcast(I32))
 
-        steps = [(g, c) for g in range(NG) for c in range(S // CHUNK)]
+        steps = [(g, lo, CHUNK) for g in range(NG) for lo in range(0, S, CHUNK)]
+        steps[-1:] = [(NG - 1, lo, CHUNK // 2) for lo in range(S - CHUNK, S, CHUNK // 2)]
         diffs, rounded = {}, {}
         for n in range(len(steps) + 2):
             if n < len(steps):
                 diffs[n] = differences(*steps[n])
             if 1 <= n <= len(steps):
-                rounded[n - 1] = scale_and_round(*steps[n - 1], diffs[n - 1])
+                copy = nc.vector.tensor_copy if n == len(steps) else nc.scalar.copy
+                rounded[n - 1] = scale_and_round(*steps[n - 1], diffs[n - 1], copy)
             if n >= 2:
                 quantise_y(*steps[n - 2], rounded[n - 2])

@@ -32,7 +32,7 @@ def tile_list_sign_phrase_encoder_kernel(
     nc = tc.nc
     with ExitStack() as ctx:
         keep = ctx.enter_context(tc.tile_pool(name="keep", bufs=1))
-        raw = ctx.enter_context(tc.tile_pool(name="raw", bufs=2))
+        raw = ctx.enter_context(tc.tile_pool(name="raw", bufs=1))
         work = ctx.enter_context(tc.tile_pool(name="work", bufs=2))
         ring = ctx.enter_context(tc.tile_pool(name="ring", bufs=3))
         psum = ctx.enter_context(tc.psum_pool(name="psum", bufs=2))
@@ -65,30 +65,31 @@ def tile_list_sign_phrase_encoder_kernel(
         nc.gpsimd.memset(w2s_raw[:].bitcast(I32), 0)
         nc.vector.memset(tab_s[:].bitcast(I32), 0)
         for q in range(4):
-            nc.scalar.dma_start(out=w2s_raw[32 * q : 32 * q + 4, :].bitcast(I32), in_=w2_scales[0, 4 * q : 4 * q + 4, :].bitcast(I32))
+            nc.gpsimd.dma_start(out=w2s_raw[32 * q : 32 * q + 4, :].bitcast(I32), in_=w2_scales[0, 4 * q : 4 * q + 4, :].bitcast(I32))
 
         def load_rows(dst, src):
             nc.sync.dma_start(out=dst, in_=src.rearrange("(p j) c -> p j c", j=PACK))
 
-        def quantise_weight(n, g, copy, w_raw, pieces):
+        def quantise_weight(n, g, copy, parts, calls):
             w_bf = work.tile([P, PACK * GROUP], BF16, name="w_bf", align_bytes=64)
             dealt = w_bf[:].rearrange("p (t m j) -> p m j t", t=PACK, j=PACK)
-            given = w_raw.rearrange("p j (m t) -> p m j t", t=PACK)
-            for u in range(pieces):
-                ms = slice(u * P // pieces, (u + 1) * P // pieces)
-                copy(out=dealt[:, ms], in_=given[:, ms])
-            nc.vector.quantize_mx(out=wq[n, g][:].bitcast(FP8X4), scales=wsc[n, g][:], in_=w_bf[:])
+            step = P // len(parts)
+            for u, given in enumerate(parts):
+                copy(out=dealt[:, u * step : (u + 1) * step], in_=given.rearrange("p j (m t) -> p m j t", t=PACK))
+            width = GROUP // calls
+            for lo in range(0, GROUP, width):
+                nc.vector.quantize_mx(
+                    out=wq[n, g][:, lo : lo + width].bitcast(FP8X4), scales=wsc[n, g][:, lo : lo + width], in_=w_bf[:, PACK * lo : PACK * (lo + width)]
+                )
 
         nc.sync.dma_start(offs_sb[:], offs)
         nc.sync.dma_start(pos1_sb[:], pos1)
         nc.sync.dma_start(pos2_sb[:], pos2)
         nc.sync.dma_start(pos3_sb[:], pos3)
-        w2_raw = kept([P, 2 * H], U8, "w2_raw")
+        w2_raw = kept([P, 2 * H], U8, "stage")
         nc.sync.dma_start(out=w2_raw[:].bitcast(I32), in_=w2_words[0].bitcast(I32))
         w1_raw0 = raw.tile([P, PACK, GROUP], F32, name="w_raw")
         load_rows(w1_raw0[:], w1[:, :GROUP])
-        w3_raw0 = raw.tile([P, PACK, GROUP], F32, name="w_raw")
-        load_rows(w3_raw0[:], w3[:, :GROUP])
         tab_w = kept([P, T], U32, "big")
         nc.sync.dma_start(out=tab_w[:].bitcast(I32), in_=tab_words[0].rearrange("p n i -> p (n i)").bitcast(I32))
         for q in range(4):
@@ -100,20 +101,21 @@ def tile_list_sign_phrase_encoder_kernel(
                 in_=src.rearrange("p (g m t) -> p g m t", g=NG, t=PACK),
             )
 
-        for g in range(NG):
-            cols = slice(2 * g * GROUP, 2 * (g + 1) * GROUP)
-            nc.vector.tensor_copy(
-                out=w2_q[:, cols].rearrange("p (t m b) -> p m t b", t=PACK, b=2),
-                in_=w2_raw[:, cols].rearrange("p (m t b) -> p m t b", t=PACK, b=2),
-            )
-        quantise_weight(1, 0, nc.vector.tensor_copy, w1_raw0[:], 1)
-        quantise_weight(3, 0, nc.vector.tensor_copy, w3_raw0[:], 1)
+        nc.scalar.copy(
+            out=w2_q[:].bitcast(U16).rearrange("p (g t m) -> p g m t", g=NG, t=PACK),
+            in_=w2_raw[:].bitcast(U16).rearrange("p (g m t) -> p g m t", g=NG, t=PACK),
+        )
+        w3_raw0 = kept([P, 2, PACK, GROUP // 2], F32, "stage")
+        for u in range(2):
+            load_rows(w3_raw0[:, u], w3[:, u * GROUP // 2 : (u + 1) * GROUP // 2])
+        quantise_weight(1, 0, nc.vector.tensor_copy, [w1_raw0[:]], 1)
         det = {}
         nc.vector.tensor_copy(v_s[:], tab_s[:].indirect(offs_sb[:]))
         deal_scales(w2_s[:], w2s_raw[:])
         for c in range(S // BANK):
             lo = c * BANK
             nc.vector.tensor_copy(v_w[:, lo : lo + BANK], tab_w[:].indirect(offs_sb[:, lo // STRIPE : (lo + BANK) // STRIPE]))
+        quantise_weight(3, 0, nc.vector.tensor_copy, [w3_raw0[:, 0], w3_raw0[:, 1]], PACK)
         w_raw1 = kept([P, 2, PACK, GROUP], F32, "big")
         load_rows(w_raw1[:, 0], w1[:, GROUP:])
         load_rows(w_raw1[:, 1], w3[:, GROUP:])
@@ -138,8 +140,7 @@ def tile_list_sign_phrase_encoder_kernel(
                 nc.scalar.activation(out=tanh_a[:, cols], in_=a_ps[:], func=ACT.Tanh)
                 nc.scalar.activation(out=silu_b[:, cols], in_=b_ps[:], func=ACT.Silu)
                 if i < 2:
-                    engine = nc.vector if i == 0 else nc.gpsimd
-                    engine.tensor_tensor(out=part[i % 3][:, cols], in0=tanh_a[:, cols], in1=silu_b[:, cols], op=ALU.mult)
+                    nc.gpsimd.tensor_tensor(out=part[i % 3][:, cols], in0=tanh_a[:, cols], in1=silu_b[:, cols], op=ALU.mult)
             if i >= 2:
                 nc.gpsimd.tensor_tensor(out=part[i % 3][:], in0=tanh_a[:], in1=silu_b[:], op=ALU.mult)
 
@@ -192,9 +193,9 @@ def tile_list_sign_phrase_encoder_kernel(
             if i > 0:
                 add_end(i - 1)
             if i == 0:
-                quantise_weight(1, 1, nc.scalar.copy, w_raw1[:, 0], 2)
+                quantise_weight(1, 1, nc.scalar.copy, [w_raw1[:, 0, :, :256], w_raw1[:, 0, :, 256:]], 1)
             if i == 1:
-                quantise_weight(3, 1, nc.scalar.copy, w_raw1[:, 1], 2)
+                quantise_weight(3, 1, nc.scalar.copy, [w_raw1[:, 1, :, :256], w_raw1[:, 1, :, 256:]], 1)
                 w4_stage = kept([P, NG * H + H // 4], I32, "big")
                 w4_raw = w4_stage[:, : NG * H].rearrange("p (a n) -> p a n", a=NG)
                 nc.vector.memset(w4_stage[:, NG * H :], 0)

@@ -32,7 +32,6 @@ def tile_list_sign_phrase_encoder_kernel(
     nc = tc.nc
     with ExitStack() as ctx:
         keep = ctx.enter_context(tc.tile_pool(name="keep", bufs=1))
-        raw = ctx.enter_context(tc.tile_pool(name="raw", bufs=1))
         work = ctx.enter_context(tc.tile_pool(name="work", bufs=2))
         ring = ctx.enter_context(tc.tile_pool(name="ring", bufs=3))
         psum = ctx.enter_context(tc.psum_pool(name="psum", bufs=2))
@@ -45,7 +44,6 @@ def tile_list_sign_phrase_encoder_kernel(
         pos2_sb = kept([P, NP // STRIPE], U16, "pos2_sb")
         pos3_sb = kept([P, S // STRIPE], U16, "pos3_sb")
         tab_s = kept([P, T], U8, "tab_s")
-        v_w = kept([P, S], U32, "v_w")
         v_s = kept([P, S], U8, "v_s")
         w2_s = kept([P, H], U8, "w2_s")
         w4_s = kept([P, H], U8, "w4_s")
@@ -61,11 +59,9 @@ def tile_list_sign_phrase_encoder_kernel(
         y_q = [kept([P, S], U32, "y_q%d" % g) for g in range(NG)]
         y_s = [kept([P, S], U8, "y_s%d" % g) for g in range(NG)]
 
-        w2s_raw = kept([P, H], U8, "small")
-        nc.gpsimd.memset(w2s_raw[:].bitcast(I32), 0)
+        w2s_raw = kept([P, H], U8, "w2s_raw")
         nc.vector.memset(tab_s[:].bitcast(I32), 0)
-        for q in range(4):
-            nc.gpsimd.dma_start(out=w2s_raw[32 * q : 32 * q + 4, :].bitcast(I32), in_=w2_scales[0, 4 * q : 4 * q + 4, :].bitcast(I32))
+        nc.gpsimd.memset(w2s_raw[:].bitcast(I32), 0)
 
         def load_rows(dst, src):
             nc.sync.dma_start(out=dst, in_=src.rearrange("(p j) c -> p j c", j=PACK))
@@ -82,18 +78,23 @@ def tile_list_sign_phrase_encoder_kernel(
                     out=wq[n, g][:, lo : lo + width].bitcast(FP8X4), scales=wsc[n, g][:, lo : lo + width], in_=w_bf[:, PACK * lo : PACK * (lo + width)]
                 )
 
+        for q in range(4):
+            nc.sync.dma_start(out=tab_s[32 * q : 32 * q + 4, :].bitcast(I32), in_=tab_scales[0, 4 * q : 4 * q + 4, :].bitcast(I32))
         nc.sync.dma_start(offs_sb[:], offs)
-        nc.sync.dma_start(pos1_sb[:], pos1)
-        nc.sync.dma_start(pos2_sb[:], pos2)
-        nc.sync.dma_start(pos3_sb[:], pos3)
-        w2_raw = kept([P, 2 * H], U8, "stage")
+        w2_raw = kept([P, 2 * H], U8, "w2_raw")
         nc.sync.dma_start(out=w2_raw[:].bitcast(I32), in_=w2_words[0].bitcast(I32))
-        w1_raw0 = raw.tile([P, PACK, GROUP], F32, name="w_raw")
+        w1_raw0 = kept([P, PACK, GROUP], F32, "w1_raw0")
         load_rows(w1_raw0[:], w1[:, :GROUP])
+        nc.sync.dma_start(pos1_sb[:], pos1)
         tab_w = kept([P, T], U32, "big")
         nc.sync.dma_start(out=tab_w[:].bitcast(I32), in_=tab_words[0].rearrange("p n i -> p (n i)").bitcast(I32))
         for q in range(4):
-            nc.scalar.dma_start(out=tab_s[32 * q : 32 * q + 4, :].bitcast(I32), in_=tab_scales[0, 4 * q : 4 * q + 4, :].bitcast(I32))
+            nc.sync.dma_start(out=w2s_raw[32 * q : 32 * q + 4, :].bitcast(I32), in_=w2_scales[0, 4 * q : 4 * q + 4, :].bitcast(I32))
+        w3_raw0 = kept([P, 2, PACK, GROUP // 2], F32, "w3_raw0")
+        for u in range(2):
+            load_rows(w3_raw0[:, u], w3[:, u * GROUP // 2 : (u + 1) * GROUP // 2])
+        nc.sync.dma_start(pos2_sb[:], pos2)
+        nc.sync.dma_start(pos3_sb[:], pos3)
 
         def deal_scales(dst, src):
             nc.vector.tensor_copy(
@@ -101,17 +102,17 @@ def tile_list_sign_phrase_encoder_kernel(
                 in_=src.rearrange("p (g m t) -> p g m t", g=NG, t=PACK),
             )
 
-        nc.scalar.copy(
-            out=w2_q[:].bitcast(U16).rearrange("p (g t m) -> p g m t", g=NG, t=PACK),
-            in_=w2_raw[:].bitcast(U16).rearrange("p (g m t) -> p g m t", g=NG, t=PACK),
-        )
-        w3_raw0 = kept([P, 2, PACK, GROUP // 2], F32, "stage")
-        for u in range(2):
-            load_rows(w3_raw0[:, u], w3[:, u * GROUP // 2 : (u + 1) * GROUP // 2])
+        for g in range(NG):
+            cols = slice(2 * g * GROUP, 2 * (g + 1) * GROUP)
+            nc.vector.tensor_copy(
+                out=w2_q[:, cols].rearrange("p (t m b) -> p m t b", t=PACK, b=2),
+                in_=w2_raw[:, cols].rearrange("p (m t b) -> p m t b", t=PACK, b=2),
+            )
         quantise_weight(1, 0, nc.vector.tensor_copy, [w1_raw0[:]], 1)
         det = {}
         nc.vector.tensor_copy(v_s[:], tab_s[:].indirect(offs_sb[:]))
         deal_scales(w2_s[:], w2s_raw[:])
+        v_w = kept([P, S], U32, "w2s_raw")
         for c in range(S // BANK):
             lo = c * BANK
             nc.vector.tensor_copy(v_w[:, lo : lo + BANK], tab_w[:].indirect(offs_sb[:, lo // STRIPE : (lo + BANK) // STRIPE]))
@@ -133,12 +134,12 @@ def tile_list_sign_phrase_encoder_kernel(
                 cols = slice(c * BANK, (c + 1) * BANK)
                 a_ps = psum.tile([P, BANK], F32, name="a_ps")
                 b_ps = psum.tile([P, BANK], F32, name="b_ps")
-                nc.tensor.matmul_mx(out=a_ps[:], lhsT=wq[1, g][:, rows].bitcast(FP8X4), lhsT_scale=wsc[1, g][:, rows], **moving(c))
                 nc.tensor.matmul_mx(
                     out=b_ps[:], lhsT=w2_q[:, 2 * i * P : 2 * (i + 1) * P].bitcast(FP4X4), lhsT_scale=w2_s[:, i * P : (i + 1) * P], **moving(c)
                 )
-                nc.scalar.activation(out=tanh_a[:, cols], in_=a_ps[:], func=ACT.Tanh)
+                nc.tensor.matmul_mx(out=a_ps[:], lhsT=wq[1, g][:, rows].bitcast(FP8X4), lhsT_scale=wsc[1, g][:, rows], **moving(c))
                 nc.scalar.activation(out=silu_b[:, cols], in_=b_ps[:], func=ACT.Silu)
+                nc.scalar.activation(out=tanh_a[:, cols], in_=a_ps[:], func=ACT.Tanh)
                 if i < 2:
                     nc.gpsimd.tensor_tensor(out=part[i % 3][:, cols], in0=tanh_a[:, cols], in1=silu_b[:, cols], op=ALU.mult)
             if i >= 2:

from contextlib import ExitStack

import concourse.mybir as mybir

K, H, T, S, NP = 512, 1024, 4096, 1024, 512
FLOPS = 2 * (3 * K * H * S + H * H * NP)

F32 = mybir.dt.float32
BF16 = mybir.dt.bfloat16
I32 = mybir.dt.int32
U32 = mybir.dt.uint32
U16 = mybir.dt.uint16
U8 = mybir.dt.uint8
FP8X4 = mybir.dt.float8_e4m3fn_x4
FP4X4 = mybir.dt.float4_e2m1fn_x4
ACT = mybir.ActivationFunctionType
ALU = mybir.AluOpType

P = 128
PACK = 4
GROUP = P * PACK
NG = H // GROUP
BANK = 512
CHUNK = 256
STRIPE = 16


def tile_list_sign_phrase_encoder_kernel(
    tc, tab_words, tab_scales, offs, pos1, pos2, pos3, w1, w2_words, w2_scales, w3, w4_words, w4_scales, detail,
    out_0, out_1, out_2,
):
    nc = tc.nc
    with ExitStack() as ctx:
        keep = ctx.enter_context(tc.tile_pool(name="keep", bufs=1))
        work = ctx.enter_context(tc.tile_pool(name="work", bufs=2))
        ring = ctx.enter_context(tc.tile_pool(name="ring", bufs=3))
        psum = ctx.enter_context(tc.psum_pool(name="psum", bufs=2))

        def kept(shape, dtype, name):
            return keep.tile(shape, dtype, name=name, align_bytes=64)

        offs_sb = kept([P, S // STRIPE], U16, "offs_sb")
        pos1_sb = kept([P, NP // STRIPE], U16, "pos1_sb")
        pos2_sb = kept([P, NP // STRIPE], U16, "pos2_sb")
        pos3_sb = kept([P, S // STRIPE], U16, "pos3_sb")
        tab_s = kept([P, T], U8, "tab_s")
        v_s = kept([P, S], U8, "v_s")
        w2_s = kept([P, H], U8, "w2_s")
        w4_s = kept([P, H], U8, "w4_s")
        w2_q = kept([P, 2 * H], U8, "w2_q")
        wq = {(n, g): kept([P, GROUP], U32, "wq%d_%d" % (n, g)) for n in (1, 3) for g in range(NG)}
        wsc = {(n, g): kept([P, GROUP], U8, "wsc%d_%d" % (n, g)) for n in (1, 3) for g in range(NG)}
        w4_q = [kept([P, H], U32, "w4_q%d" % a) for a in range(NG)]
        h = [kept([P, S], F32, "h%d" % i) for i in range(NG * PACK)]
        sign = [kept([P, NP], F32, "sign%d" % i) for i in range(NG * PACK)]
        part = [kept([P, S], F32, "part%d" % n) for n in range(3)]
        x_q = [kept([P, NP], U32, "x_q%d" % g) for g in range(NG)]
        x_s = [kept([P, NP], U8, "x_s%d" % g) for g in range(NG)]
        y_q = [kept([P, S], U32, "y_q%d" % g) for g in range(NG)]
        y_s = [kept([P, S], U8, "y_s%d" % g) for g in range(NG)]

        w2s_raw = kept([P, H], U8, "w2s_raw")
        nc.vector.memset(tab_s[:].bitcast(I32), 0)
        nc.gpsimd.memset(w2s_raw[:].bitcast(I32), 0)

        def load_rows(dst, src):
            nc.sync.dma_start(out=dst, in_=src.rearrange("(p j) c -> p j c", j=PACK))

        def quantise_weight(n, g, copy, parts, calls):
            w_bf = work.tile([P, PACK * GROUP], BF16, name="w_bf", align_bytes=64)
            dealt = w_bf[:].rearrange("p (t m j) -> p m j t", t=PACK, j=PACK)
            step = P // len(parts)
            for u, given in enumerate(parts):
                copy(out=dealt[:, u * step : (u + 1) * step], in_=given.rearrange("p j (m t) -> p m j t", t=PACK))
            width = GROUP // calls
            for lo in range(0, GROUP, width):
                nc.vector.quantize_mx(
                    out=wq[n, g][:, lo : lo + width].bitcast(FP8X4), scales=wsc[n, g][:, lo : lo + width], in_=w_bf[:, PACK * lo : PACK * (lo + width)]
                )

        for q in range(4):
            nc.sync.dma_start(out=tab_s[32 * q : 32 * q + 4, :].bitcast(I32), in_=tab_scales[0, 4 * q : 4 * q + 4, :].bitcast(I32))
        nc.sync.dma_start(offs_sb[:], offs)
        w2_raw = kept([P, 2 * H], U8, "w2_raw")
        nc.sync.dma_start(out=w2_raw[:].bitcast(I32), in_=w2_words[0].bitcast(I32))
        w1_raw0 = kept([P, PACK, GROUP], F32, "w1_raw0")
        load_rows(w1_raw0[:], w1[:, :GROUP])
        nc.sync.dma_start(pos1_sb[:], pos1)
        tab_w = kept([P, T], U32, "big")
        nc.sync.dma_start(out=tab_w[:].bitcast(I32), in_=tab_words[0].rearrange("p n i -> p (n i)").bitcast(I32))
        for q in range(4):
            nc.sync.dma_start(out=w2s_raw[32 * q : 32 * q + 4, :].bitcast(I32), in_=w2_scales[0, 4 * q : 4 * q + 4, :].bitcast(I32))
        w3_raw0 = kept([P, 2, PACK, GROUP // 2], F32, "w3_raw0")
        for u in range(2):
            load_rows(w3_raw0[:, u], w3[:, u * GROUP // 2 : (u + 1) * GROUP // 2])
        nc.sync.dma_start(pos2_sb[:], pos2)
        nc.sync.dma_start(pos3_sb[:], pos3)

        def deal_scales(dst, src):
            nc.vector.tensor_copy(
                out=dst.rearrange("p (g t m) -> p g m t", g=NG, t=PACK),
                in_=src.rearrange("p (g m t) -> p g m t", g=NG, t=PACK),
            )

        for g in range(NG):
            cols = slice(2 * g * GROUP, 2 * (g + 1) * GROUP)
            nc.vector.tensor_copy(
                out=w2_q[:, cols].rearrange("p (t m b) -> p m t b", t=PACK, b=2),
                in_=w2_raw[:, cols].rearrange("p (m t b) -> p m t b", t=PACK, b=2),
            )
        quantise_weight(1, 0, nc.vector.tensor_copy, [w1_raw0[:]], 1)
        det = {}
        nc.vector.tensor_copy(v_s[:], tab_s[:].indirect(offs_sb[:]))
        deal_scales(w2_s[:], w2s_raw[:])
        v_w = kept([P, S], U32, "w2s_raw")
        for c in range(S // BANK):
            lo = c * BANK
            nc.vector.tensor_copy(v_w[:, lo : lo + BANK], tab_w[:].indirect(offs_sb[:, lo // STRIPE : (lo + BANK) // STRIPE]))
        quantise_weight(3, 0, nc.vector.tensor_copy, [w3_raw0[:, 0], w3_raw0[:, 1]], PACK)
        w_raw1 = kept([P, 2, PACK, GROUP], F32, "big")
        load_rows(w_raw1[:, 0], w1[:, GROUP:])
        load_rows(w_raw1[:, 1], w3[:, GROUP:])

        def moving(c):
            cols = slice(c * BANK, (c + 1) * BANK)
            return dict(rhs=v_w[:, cols].bitcast(FP8X4), rhs_scale=v_s[:, cols], start=True, stop=True)

        def gates(i):
            g, t = divmod(i, PACK)
            rows = slice(t * P, (t + 1) * P)
            tanh_a = work.tile([P, S], F32, name="tanh_a")
            silu_b = work.tile([P, S], F32, name="silu_b")
            for c in range(S // BANK):
                cols = slice(c * BANK, (c + 1) * BANK)
                a_ps = psum.tile([P, BANK], F32, name="a_ps")
                b_ps = psum.tile([P, BANK], F32, name="b_ps")
                nc.tensor.matmul_mx(
                    out=b_ps[:], lhsT=w2_q[:, 2 * i * P : 2 * (i + 1) * P].bitcast(FP4X4), lhsT_scale=w2_s[:, i * P : (i + 1) * P], **moving(c)
                )
                nc.tensor.matmul_mx(out=a_ps[:], lhsT=wq[1, g][:, rows].bitcast(FP8X4), lhsT_scale=wsc[1, g][:, rows], **moving(c))
                nc.scalar.activation(out=silu_b[:, cols], in_=b_ps[:], func=ACT.Silu)
                nc.scalar.activation(out=tanh_a[:, cols], in_=a_ps[:], func=ACT.Tanh)
                if i < 2:
                    nc.gpsimd.tensor_tensor(out=part[i % 3][:, cols], in0=tanh_a[:, cols], in1=silu_b[:, cols], op=ALU.mult)
            if i >= 2:
                nc.gpsimd.tensor_tensor(out=part[i % 3][:], in0=tanh_a[:], in1=silu_b[:], op=ALU.mult)

        def finish_h(i, c):
            g, t = divmod(i, PACK)
            rows = slice(t * P, (t + 1) * P)
            cols = slice(c * BANK, (c + 1) * BANK)
            c_ps = psum.tile([P, BANK], F32, name="c_ps")
            nc.tensor.matmul_mx(out=c_ps[:], lhsT=wq[3, g][:, rows].bitcast(FP8X4), lhsT_scale=wsc[3, g][:, rows], **moving(c))
            nc.vector.tensor_tensor(out=h[i][:, cols], in0=c_ps[:], in1=part[i % 3][:, cols], op=ALU.mult)

        x_f = {}

        def pick_start(i, lo=0, hi=NP):
            nc.vector.tensor_copy(part[i % 3][:, lo:hi], h[i][:].indirect(pos1_sb[:, lo // STRIPE : hi // STRIPE]))

        def add_end(i, lo=0, hi=NP):
            g, t = divmod(i, PACK)
            if t == 0:
                x_f[g] = keep.tile([P, PACK, NP], F32, name="x_f")
            nc.vector.tensor_tensor(
                out=x_f[g][:, t, lo:hi], in0=h[i][:].indirect(pos2_sb[:, lo // STRIPE : hi // STRIPE]), in1=part[i % 3][:, lo:hi], op=ALU.add
            )

        def interleave(copy, dst, src):
            copy(out=dst.rearrange("p (c i t) -> p c t i", i=4, t=PACK), in_=src.rearrange("p t (c i) -> p c t i", i=4))

        def quantise_x(g, copies):
            for c in range(NP // CHUNK):
                cols = slice(c * CHUNK, (c + 1) * CHUNK)
                x_bf = work.tile([P, PACK * CHUNK], BF16, name="x_bf", align_bytes=64)
                interleave(copies[c], x_bf[:], x_f[g][:, :, cols])
                nc.vector.quantize_mx(out=x_q[g][:, cols].bitcast(FP8X4), scales=x_s[g][:, cols], in_=x_bf[:])

        def deal_w4(w4_raw, a):
            nc.scalar.copy(
                out=w4_q[a][:].rearrange("p (g t m) -> p g m t", g=NG, t=PACK),
                in_=w4_raw[:, a, :].bitcast(U32).rearrange("p (g m t) -> p g m t", g=NG, t=PACK),
            )

        n_tiles = NG * PACK
        gates(0)
        for i in range(n_tiles):
            if i + 1 < n_tiles:
                gates(i + 1)
            finish_h(i, 0)
            if i > 0:
                pick_start(i - 1)
            finish_h(i, 1)
            if i > 0:
                add_end(i - 1)
            if i == 0:
                quantise_weight(1, 1, nc.scalar.copy, [w_raw1[:, 0, :, :256], w_raw1[:, 0, :, 256:]], 1)
            if i == 1:
                quantise_weight(3, 1, nc.scalar.copy, [w_raw1[:, 1, :, :256], w_raw1[:, 1, :, 256:]], 1)
                w4_stage = kept([P, NG * H + H // 4], I32, "big")
                w4_raw = w4_stage[:, : NG * H].rearrange("p (a n) -> p a n", a=NG)
                nc.vector.memset(w4_stage[:, NG * H :], 0)
                nc.sync.dma_start(out=w4_raw, in_=w4_words.rearrange("a p n i -> p a (n i)").bitcast(I32))
                for q in range(4):
                    nc.sync.dma_start(out=w4_stage[32 * q : 32 * q + 8, NG * H :], in_=w4_scales[:, 4 * q : 4 * q + 4, :].bitcast(I32))
            if i == 2:
                deal_scales(w4_s[:], w4_stage[:, NG * H :].bitcast(U8))
                for u in range(2):
                    det[0, u] = work.tile([P, PACK, BANK], F32, name="w_bf", align_bytes=64)
                    load_rows(det[0, u][:], detail[:GROUP, u * BANK : (u + 1) * BANK])
            if i in (2, 3):
                deal_w4(w4_raw, i - 2)
            if i == 3:
                det1 = kept([P, 2, PACK, BANK], F32, "big")
                for u in range(2):
                    det[1, u] = det1[:, u]
                    load_rows(det[1, u], detail[GROUP:, u * BANK : (u + 1) * BANK])
            if i == PACK:
                quantise_x(0, [nc.scalar.copy, nc.scalar.copy])
        for lo in range(0, NP, CHUNK):
            pick_start(n_tiles - 1, lo, lo + CHUNK)
        for lo in range(0, NP, CHUNK):
            add_end(n_tiles - 1, lo, lo + CHUNK)
        quantise_x(1, [nc.scalar.copy, nc.vector.tensor_copy])

        for i in range(n_tiles):
            rows = slice(i * P, (i + 1) * P)
            s_ps = psum.tile([P, NP], F32, name="s_ps")
            for a in range(NG):
                nc.tensor.matmul_mx(
                    out=s_ps[:], lhsT=w4_q[a][:, rows].bitcast(FP8X4), lhsT_scale=w4_s[4 * a :, rows],
                    rhs=x_q[a][:].bitcast(FP8X4), rhs_scale=x_s[a][:], start=(a == 0), stop=(a == NG - 1),
                )
            nc.scalar.copy(out=sign[i][:], in_=s_ps[:])

        def differences(g, lo, width):
            diff = work.tile([P, PACK, width], F32, name="diff")
            places = pos3_sb[:, lo // STRIPE : (lo + width) // STRIPE]
            for t in range(PACK):
                i = g * PACK + t
                nc.vector.tensor_tensor(out=diff[:, t, :], in0=sign[i][:].indirect(places), in1=h[i][:, lo : lo + width], op=ALU.subtract)
            return diff

        def scale_and_round(g, lo, width, diff, copy):
            y = ring.tile([P, PACK, width], F32, name="y")
            u, at = divmod(lo, BANK)
            nc.vector.tensor_tensor(out=y[:], in0=diff[:], in1=det[g, u][:, :, at : at + width], op=ALU.mult)
            nc.sync.dma_start(out=out_0[g * GROUP : (g + 1) * GROUP, lo : lo + width].rearrange("(p t) c -> p t c", t=PACK), in_=y[:])
            y_bf = work.tile([P, PACK * width], BF16, name="y_bf", align_bytes=64)
            interleave(copy, y_bf[:], y[:])
            return y_bf

        def quantise_y(g, lo, width, y_bf):
            cols = slice(lo, lo + width)
            nc.vector.quantize_mx(out=y_q[g][:, cols].bitcast(FP8X4), scales=y_s[g][:, cols], in_=y_bf[:])
            nc.sync.dma_start(out=out_1[g].rearrange("p n i -> p (n i)").bitcast(I32)[:, cols], in_=y_q[g][:, cols].bitcast(I32))
            if lo + width == S:
                for q in range(4):
                    nc.scalar.dma_start(out=out_2[g, 4 * q : 4 * q + 4, :].bitcast(I32), in_=y_s[g][32 * q : 32 * q + 4, :].bitcast(I32))

        steps = [(g, lo, CHUNK) for g in range(NG) for lo in range(0, S, CHUNK)]
        steps[-1:] = [(NG - 1, lo, CHUNK // 2) for lo in range(S - CHUNK, S, CHUNK // 2)]
        diffs, rounded = {}, {}
        for n in range(len(steps) + 2):
            if n < len(steps):
                diffs[n] = differences(*steps[n])
            if 1 <= n <= len(steps):
                copy = nc.vector.tensor_copy if n == len(steps) else nc.scalar.copy
                rounded[n - 1] = scale_and_round(*steps[n - 1], diffs[n - 1], copy)
            if n >= 2:
                quantise_y(*steps[n - 2], rounded[n - 2])
